import numpy as np
import ml_dtypes


def mxq(x, axis, fmt="e4m3"):
    dtype, down = {"e4m3": (ml_dtypes.float8_e4m3fn, 7), "e5m2": (ml_dtypes.float8_e5m2, 14)}[fmt]
    v = np.moveaxis(np.asarray(x, np.float32).astype(ml_dtypes.bfloat16).astype(np.float64), axis, -1)
    blocks = v.reshape(v.shape[:-1] + (-1, 32))
    amax = np.abs(blocks).max(-1, keepdims=True)
    byte = np.maximum(np.where(amax > 0, np.frexp(amax)[1] - 1 + 127, 0) - down, 1)
    scale = np.exp2(byte - 127.0)
    codes = (blocks / scale).astype(np.float32).astype(dtype).astype(np.float64)
    return np.moveaxis((codes * scale).reshape(v.shape), -1, axis)


WIDE = False


def mx_kscale(k):
    if not WIDE:
        return np.ones(k)
    levels = np.array([10, -10, 5, -5, 0])
    if k % 512:
        return np.exp2(np.random.permutation(np.resize(levels, k // 32))).repeat(32)
    a = np.empty((k // 512, 16))
    for p in range(k // 512):
        a[p, :8] = np.random.permutation(np.resize(levels, 8))
        for g in range(8):
            far = levels[np.abs(levels - a[p, g]) >= 10]
            a[p, g + 8] = far[np.random.randint(len(far))]
    return np.exp2(a.ravel()).repeat(32)


def f64(x):
    return np.asarray(x).astype(np.float64)


def striped(idx):
    return np.tile(idx.reshape(-1, 16).T, (8, 1)).astype(np.uint16)


def unstriped(offs):
    return offs[:16].T.reshape(-1).astype(np.int64)


def pack_weight(w):
    k, n = w.shape
    w = f64(np.asarray(w, np.float32).astype(ml_dtypes.bfloat16)).reshape(k // 32, 32, n)
    amax = np.abs(w).max(1)
    byte = np.clip(np.where(amax > 0, np.frexp(amax)[1] - 1 + 127 - 7, 1), 1, 254)
    scaled = (w * np.exp2(127.0 - byte)[:, None, :]).reshape(k, n).astype(np.float32)
    words = np.ascontiguousarray(scaled.reshape(k // 512, 128, 4, n).transpose(0, 1, 3, 2)).astype(ml_dtypes.float8_e4m3fn).view(np.uint8)
    return words, np.ascontiguousarray(byte.astype(np.uint8).reshape(k // 512, 16, n))


def unpack_weight(words, scales):
    g, p, n, _ = words.shape
    vals = np.ascontiguousarray(words).view(ml_dtypes.float8_e4m3fn).astype(np.float64) * np.repeat(np.exp2(scales.astype(np.float64) - 127.0), 8, axis=1)[..., None]
    return vals.transpose(0, 1, 3, 2).reshape(g * 512, n)


K, T, S, N, H, V, U = 1024, 2048, 512, 128, 512, 256, 1024


def setup_inputs():
    n = np.random.standard_normal
    s = mx_kscale(K)[:, None]
    u = mx_kscale(H)
    packed_xT = pack_weight(n((K, T)) * s)
    return {
        "x_words": packed_xT[0],
        "x_scales": packed_xT[1],
        "w1": (n((K, H)) / np.sqrt(K) / s).astype(np.float32),
        "w2": (n((K, H)) / np.sqrt(K) / s).astype(np.float32),
        "pr": (np.random.uniform(0.3, 1.7, (H, U))).astype(np.float32),
        "unit": (np.random.uniform(0.6, 1.4, (H, 1)) * u[:, None]).astype(np.float32),
        "w3": (n((H, N)) / np.sqrt(H) / u[:, None]).astype(np.float32),
        "offs": striped(np.random.permutation(T)[:S]),
        "kept": striped(np.random.permutation(S)[:V]),
        "drop1": striped(np.random.permutation(S)[:V]),
        "drop2": striped(np.random.permutation(S)[:V]),
        "rd": striped(np.random.permutation(np.concatenate([np.arange(V), np.random.randint(0, V, U - V)]))),
    }


def reference(x_words, x_scales, w1, w2, pr, unit, w3, offs, kept, drop1, drop2, rd):
    xq = unpack_weight(x_words, x_scales)[:, unstriped(offs)]
    yv = mxq(f64(w2), 0, "e4m3").T @ xq
    y = mxq(f64(w1), 0, "e4m3").T @ xq
    y_drop1 = y[:, unstriped(drop1)]
    kk = y[:, unstriped(kept)]
    w_drop1 = np.exp(np.tanh(y_drop1 * kk))
    y_drop2 = y[:, unstriped(drop2)]
    w_drop2 = np.exp(np.tanh(y_drop2 * kk))
    den = w_drop1 + w_drop2 + 2.0
    mv = (2.0 * yv[:, unstriped(kept)] + w_drop1 * yv[:, unstriped(drop1)] + w_drop2 * yv[:, unstriped(drop2)]) / den
    mr = mv[:, unstriped(rd)]
    hid = f64(unit) * (mr * f64(pr))
    return mxq(f64(w3), 0, "e4m3").T @ mxq(hid, 0, "e4m3")

@@ -1,0 +1,227 @@
+from contextlib import ExitStack
+
+import math
+
+import concourse.mybir as mybir
+from concourse.masks import make_identity
+
+K, T, S, N, H, V, U = 1024, 2048, 512, 128, 512, 256, 1024
+FLOPS = 2 * (2 * K * H * S + H * N * U)
+
+F32 = mybir.dt.float32
+BF16 = mybir.dt.bfloat16
+I32 = mybir.dt.int32
+U32 = mybir.dt.uint32
+U16 = mybir.dt.uint16
+U8 = mybir.dt.uint8
+FP8X4 = mybir.dt.float8_e4m3fn_x4
+ACT = mybir.ActivationFunctionType
+ALU = mybir.AluOpType
+
+P = 128
+PACK = 4
+PASSES = K // (P * PACK)
+CHUNKS = (512, 256, 128, 128)
+WINDOW = max(CHUNKS) + 16
+
+
+def tile_picked_ywvmrg_read_p_kernel(tc, x_words, x_scales, w1, w2, pr, unit, w3, offs, kept, drop1, drop2, rd, out):
+    nc = tc.nc
+    with ExitStack() as ctx:
+        lists = ctx.enter_context(tc.tile_pool(name="lists", bufs=1))
+        keep = ctx.enter_context(tc.tile_pool(name="keep", bufs=1))
+        ring = ctx.enter_context(tc.tile_pool(name="ring", bufs=2))
+        mm = ctx.enter_context(tc.psum_pool(name="mm", bufs=4))
+        sums = ctx.enter_context(tc.psum_pool(name="sums", bufs=1))
+
+        def load_list(src, name):
+            tile = lists.tile(list(src.shape), U16, name=name)
+            nc.sync.dma_start(tile[:], src)
+            return tile
+
+        def by_slot(src):
+            return src.rearrange("(b t i) n -> t b i n", t=PACK, i=8)
+
+        scale_win = keep.tile([P, T], U8, name="scale_win", align_bytes=64)
+        nc.vector.memset(scale_win[:].bitcast(I32), 0)
+        for q in range(4):
+            nc.scalar.dma_start(scale_win[32 * q : 32 * q + 8, :].bitcast(I32), x_scales[:, 4 * q : 4 * q + 4, :].bitcast(I32))
+
+        def load_words(o):
+            win = keep.tile([P, T], I32, name=f"word_win{o}", align_bytes=64)
+            nc.sync.dma_start(win[:], x_words[o].rearrange("p c r -> p (c r)").bitcast(I32))
+            return win
+
+        word_win = [load_words(0)]
+        offs_t = load_list(offs, "offs_t")
+        kept_t = load_list(kept, "kept_t")
+        drop1_t = load_list(drop1, "drop1_t")
+        drop2_t = load_list(drop2, "drop2_t")
+        rd_t = load_list(rd, "rd_t")
+        word_win.append(load_words(1))
+
+        def load_weight(w, name):
+            raws = []
+            for o in range(PASSES):
+                raw = keep.tile([P, PACK, H], F32, name=f"{name}_raw{o}")
+                nc.sync.dma_start(raw[:], w[512 * o : 512 * (o + 1), :].rearrange("(p j) c -> p j c", j=PACK))
+                raws.append(raw)
+            return raws
+
+        w1_raw = load_weight(w1, "w1")
+        w2_raw = load_weight(w2, "w2")
+        unit_t = []
+        with nc.allow_non_contiguous_dma(reason="one value a partition"):
+            for t in range(PACK):
+                tile = keep.tile([P, 1], F32, name=f"unit{t}")
+                nc.sync.dma_start(tile[:], by_slot(unit)[t])
+                unit_t.append(tile)
+        pr_t = []
+        for t in range(PACK):
+            tile = keep.tile([P, U], F32, name=f"pr{t}")
+            nc.sync.dma_start(tile[:], by_slot(pr)[t])
+            pr_t.append(tile)
+        w3_raw = keep.tile([P, PACK, N], F32, name="w3_raw")
+        for t in range(PACK):
+            nc.sync.dma_start(w3_raw[:, t, :], by_slot(w3)[t])
+
+        ident = keep.tile([P, P], F32, name="ident")
+        make_identity(nc, ident[:])
+        mv_win = []
+        for t in range(PACK):
+            win = keep.tile([P, WINDOW], F32, name=f"mv_win{t}")
+            nc.gpsimd.memset(win[:, V:], 0.0)
+            mv_win.append(win)
+
+        x_codes = []
+        for o in range(PASSES):
+            codes = keep.tile([P, S], U32, name=f"x_codes{o}", align_bytes=64)
+            nc.vector.tensor_copy(codes[:], word_win[o][:].bitcast(U32).indirect(offs_t[:]))
+            x_codes.append(codes)
+            if o == 0:
+                x_bytes = keep.tile([P, S], U8, name="x_bytes", align_bytes=64)
+                nc.vector.tensor_copy(x_bytes[:], scale_win[:].indirect(offs_t[:]))
+
+        def cast(engine_copy, raw, t, dst):
+            src = raw[:].rearrange("p j (b t h i) -> p t b h j i", t=PACK, h=2, i=4)[:, t]
+            engine_copy(dst.rearrange("p (b h i j) -> p b h j i", h=2, i=4, j=PACK), src)
+
+        def quantise(src, width, name):
+            codes = keep.tile([P, width // PACK], U32, name=name + "_codes", align_bytes=64)
+            scales = keep.tile([P, width // PACK], U8, name=name + "_scales", align_bytes=64)
+            nc.vector.quantize_mx(out=codes[:].bitcast(FP8X4), scales=scales[:], in_=src)
+            return codes, scales
+
+        def product(acc, o, codes, scales):
+            nc.tensor.matmul_mx(out=acc[:], lhsT=codes.bitcast(FP8X4), lhsT_scale=scales, rhs=x_codes[o][:].bitcast(FP8X4),
+                                rhs_scale=x_bytes[4 * o : P, :], start=(o == 0), stop=(o == PASSES - 1))
+
+        vcopy, scopy = nc.vector.tensor_copy, nc.scalar.copy
+
+        y_acc = [mm.tile([P, S], F32, name="acc") for t in range(PACK)]
+        for o in range(PASSES):
+            for t in range(PACK):
+                grouped = keep.tile([P, P * PACK], BF16, name=f"w1_bf{o}{t}", align_bytes=64)
+                cast(vcopy if t % 2 == 0 else scopy, w1_raw[o], t, grouped[:])
+                codes, scales = quantise(grouped[:], P * PACK, f"w1_{o}{t}")
+                product(y_acc[t], o, codes[:], scales[:])
+        y_win = []
+        for t in range(PACK):
+            win = keep.tile([P, S], F32, name=f"y_win{t}")
+            (vcopy if t == 0 else scopy)(win[:], y_acc[t][:])
+            y_win.append(win)
+
+        half_w = []
+        yv_win = []
+        s_bank = [sums.tile([P, 2 * V], F32, name=f"s_bank{u}") for u in range(2)]
+
+        def keys(t):
+            kk = ring.tile([P, V], F32, name="kk")
+            prod = ring.tile([P, 2 * V], F32, name="prod")
+            nc.vector.tensor_copy(kk[:], y_win[t][:].indirect(kept_t[:]))
+            nc.vector.tensor_tensor(prod[:, :V], y_win[t][:].indirect(drop1_t[:]), kk[:], ALU.mult)
+            nc.vector.tensor_tensor(prod[:, V:], y_win[t][:].indirect(drop2_t[:]), kk[:], ALU.mult)
+            bounded = ring.tile([P, 2 * V], F32, name="bounded")
+            nc.scalar.activation(bounded[:], prod[:], ACT.Tanh)
+            hw = keep.tile([P, 2 * V], F32, name=f"half_w{t}")
+            nc.scalar.activation(hw[:], bounded[:], ACT.Exp, bias=-math.log(2.0))
+            half_w.append(hw)
+            for u in range(V // P):
+                dst = s_bank[t // 2][:, (t % 2) * V + u * P : (t % 2) * V + (u + 1) * P]
+                for d in range(2):
+                    nc.tensor.matmul(dst, lhsT=hw[:, d * V + u * P : d * V + (u + 1) * P], rhs=ident[:], is_transpose=True,
+                                     start=(d == 0), stop=(d == 1))
+
+        def value_product(t):
+            grouped = keep.tile([P, PASSES * P * PACK], BF16, name=f"w2_bf{t}", align_bytes=64)
+            for o in range(PASSES):
+                cast(scopy if t < 2 else vcopy, w2_raw[o], t, grouped[:, o * P * PACK : (o + 1) * P * PACK])
+            codes, scales = quantise(grouped[:], PASSES * P * PACK, f"w2_{t}")
+            acc = mm.tile([P, S], F32, name="acc")
+            for o in range(PASSES):
+                product(acc, o, codes[:, o * P : (o + 1) * P], scales[:, o * P : (o + 1) * P])
+            win = keep.tile([P, S], F32, name=f"yv_win{t}")
+            nc.scalar.activation(win[:], acc[:], ACT.Copy, scale=unit_t[t][:])
+            yv_win.append(win)
+
+        keys(0)
+        keys(1)
+        value_product(0)
+        keys(2)
+        value_product(1)
+        keys(3)
+        value_product(2)
+        value_product(3)
+
+        log_s = keep.tile([P, PACK * V], F32, name="log_s")
+        for u in range(2):
+            nc.scalar.activation(log_s[:, u * 2 * V : (u + 1) * 2 * V], s_bank[u][:], ACT.Ln)
+        rho = []
+        for t in range(PACK):
+            tile = keep.tile([P, V], F32, name=f"rho{t}")
+            nc.scalar.activation(tile[:], log_s[:, t * V : (t + 1) * V], ACT.Tanh, scale=0.5)
+            rho.append(tile)
+
+        def values(t):
+            terms = ring.tile([P, 3 * V], F32, name="terms")
+            nc.vector.tensor_copy(terms[:, :V], yv_win[t][:].indirect(kept_t[:]))
+            nc.vector.tensor_tensor(terms[:, V : 2 * V], yv_win[t][:].indirect(drop1_t[:]), half_w[t][:, :V], ALU.mult)
+            nc.vector.tensor_tensor(terms[:, 2 * V :], yv_win[t][:].indirect(drop2_t[:]), half_w[t][:, V:], ALU.mult)
+            n_bank = sums.tile([P, V], F32, name="n_bank")
+            for u in range(V // P):
+                for d in range(3):
+                    nc.tensor.matmul(n_bank[:, u * P : (u + 1) * P], lhsT=terms[:, d * V + u * P : d * V + (u + 1) * P], rhs=ident[:],
+                                     is_transpose=True, start=(d == 0), stop=(d == 2))
+            return n_bank
+
+        def merge(t, n_bank):
+            turned = ring.tile([P, V], F32, name="turned")
+            nc.vector.scalar_tensor_tensor(turned[:], rho[t][:], 1.0, n_bank[:], ALU.subtract, ALU.mult)
+            back = sums.tile([P, V], F32, name="back")
+            for u in range(V // P):
+                nc.tensor.transpose(back[:, u * P : (u + 1) * P], turned[:, u * P : (u + 1) * P], ident[:])
+            nc.scalar.activation(mv_win[t][:, :V], back[:], ACT.Copy, scale=-0.5)
+
+        for t in range(PACK):
+            merge(t, values(t))
+
+        w3_bf = keep.tile([P, N * PACK], BF16, name="w3_bf", align_bytes=64)
+        nc.scalar.copy(w3_bf[:].rearrange("p (c i j) -> p c j i", i=4, j=PACK), w3_raw[:].rearrange("p j (c i) -> p c j i", i=4))
+        w3_codes, w3_scales = quantise(w3_bf[:], N * PACK, "w3")
+
+        r0 = 0
+        for c, width in enumerate(CHUNKS):
+            planes = keep.tile([P, PACK, width], F32, name=f"planes{c}")
+            for t in range(PACK):
+                nc.vector.tensor_tensor(planes[:, t, :], mv_win[t][:].indirect(rd_t[:, r0 // 16 : (r0 + width) // 16]),
+                                        pr_t[t][:, r0 : r0 + width], ALU.mult)
+            hid_bf = keep.tile([P, width * PACK], BF16, name=f"hid_bf{c}", align_bytes=64)
+            nc.scalar.copy(hid_bf[:].rearrange("p (c i j) -> p c j i", i=4, j=PACK), planes[:].rearrange("p j (c i) -> p c j i", i=4))
+            codes, scales = quantise(hid_bf[:], width * PACK, f"hid{c}")
+            acc = mm.tile([P, S], F32, name="acc")
+            nc.tensor.matmul_mx(out=acc[:, :width], lhsT=w3_codes[:].bitcast(FP8X4), lhsT_scale=w3_scales[:],
+                                rhs=codes[:].bitcast(FP8X4), rhs_scale=scales[:], start=True, stop=True)
+            result = keep.tile([P, width], F32, name=f"result{c}")
+            nc.scalar.copy(result[:], acc[:, :width])
+            nc.sync.dma_start(out[:, r0 : r0 + width], result[:])
+            r0 += width

@@ -21,7 +21,7 @@ ALU = mybir.AluOpType
 P = 128
 PACK = 4
 PASSES = K // (P * PACK)
-CHUNKS = (512, 256, 128, 128)
+CHUNKS = (256, 256, 256, 128, 128)
 WINDOW = max(CHUNKS) + 16
 
 
@@ -44,8 +44,6 @@ def tile_picked_ywvmrg_read_p_kernel(tc, x_words, x_scales, w1, w2, pr, unit, w3
 
         scale_win = keep.tile([P, T], U8, name="scale_win", align_bytes=64)
         nc.vector.memset(scale_win[:].bitcast(I32), 0)
-        for q in range(4):
-            nc.scalar.dma_start(scale_win[32 * q : 32 * q + 8, :].bitcast(I32), x_scales[:, 4 * q : 4 * q + 4, :].bitcast(I32))
 
         def load_words(o):
             win = keep.tile([P, T], I32, name=f"word_win{o}", align_bytes=64)
@@ -53,11 +51,9 @@ def tile_picked_ywvmrg_read_p_kernel(tc, x_words, x_scales, w1, w2, pr, unit, w3
             return win
 
         word_win = [load_words(0)]
+        for q in range(4):
+            nc.sync.dma_start(scale_win[32 * q : 32 * q + 8, :].bitcast(I32), x_scales[:, 4 * q : 4 * q + 4, :].bitcast(I32))
         offs_t = load_list(offs, "offs_t")
-        kept_t = load_list(kept, "kept_t")
-        drop1_t = load_list(drop1, "drop1_t")
-        drop2_t = load_list(drop2, "drop2_t")
-        rd_t = load_list(rd, "rd_t")
         word_win.append(load_words(1))
 
         def load_weight(w, name):
@@ -69,18 +65,22 @@ def tile_picked_ywvmrg_read_p_kernel(tc, x_words, x_scales, w1, w2, pr, unit, w3
             return raws
 
         w1_raw = load_weight(w1, "w1")
+        kept_t = load_list(kept, "kept_t")
+        drop1_t = load_list(drop1, "drop1_t")
+        drop2_t = load_list(drop2, "drop2_t")
         w2_raw = load_weight(w2, "w2")
+        pr_t = []
+        for t in range(PACK):
+            tile = keep.tile([P, U], F32, name=f"pr{t}")
+            nc.sync.dma_start(tile[:], by_slot(pr)[t])
+            pr_t.append(tile)
+        rd_t = load_list(rd, "rd_t")
         unit_t = []
         with nc.allow_non_contiguous_dma(reason="one value a partition"):
             for t in range(PACK):
                 tile = keep.tile([P, 1], F32, name=f"unit{t}")
                 nc.sync.dma_start(tile[:], by_slot(unit)[t])
                 unit_t.append(tile)
-        pr_t = []
-        for t in range(PACK):
-            tile = keep.tile([P, U], F32, name=f"pr{t}")
-            nc.sync.dma_start(tile[:], by_slot(pr)[t])
-            pr_t.append(tile)
         w3_raw = keep.tile([P, PACK, N], F32, name="w3_raw")
         for t in range(PACK):
             nc.sync.dma_start(w3_raw[:, t, :], by_slot(w3)[t])
@@ -119,12 +119,11 @@ def tile_picked_ywvmrg_read_p_kernel(tc, x_words, x_scales, w1, w2, pr, unit, w3
         vcopy, scopy = nc.vector.tensor_copy, nc.scalar.copy
 
         y_acc = [mm.tile([P, S], F32, name="acc") for t in range(PACK)]
-        for o in range(PASSES):
-            for t in range(PACK):
-                grouped = keep.tile([P, P * PACK], BF16, name=f"w1_bf{o}{t}", align_bytes=64)
-                cast(vcopy if t % 2 == 0 else scopy, w1_raw[o], t, grouped[:])
-                codes, scales = quantise(grouped[:], P * PACK, f"w1_{o}{t}")
-                product(y_acc[t], o, codes[:], scales[:])
+        for o, t in sorted(((o, t) for o in range(PASSES) for t in range(PACK)), key=lambda ot: (ot[1] + 2 * ot[0], -ot[0])):
+            grouped = keep.tile([P, P * PACK], BF16, name=f"w1_bf{o}{t}", align_bytes=64)
+            cast(vcopy if t == 0 else scopy, w1_raw[o], t, grouped[:])
+            codes, scales = quantise(grouped[:], P * PACK, f"w1_{o}{t}")
+            product(y_acc[t], o, codes[:], scales[:])
         y_win = []
         for t in range(PACK):
             win = keep.tile([P, S], F32, name=f"y_win{t}")
@@ -133,77 +132,90 @@ def tile_picked_ywvmrg_read_p_kernel(tc, x_words, x_scales, w1, w2, pr, unit, w3
 
         half_w = []
         yv_win = []
-        s_bank = [sums.tile([P, 2 * V], F32, name=f"s_bank{u}") for u in range(2)]
+        s_bank = [sums.tile([P, 2 * V], F32, name="s_bank", bufs=2) for u in range(2)]
 
         def keys(t):
-            kk = ring.tile([P, V], F32, name="kk")
-            prod = ring.tile([P, 2 * V], F32, name="prod")
+            kk = keep.tile([P, V], F32, name=f"kk{t}")
+            prod = keep.tile([P, 2 * V], F32, name=f"prod{t}")
             nc.vector.tensor_copy(kk[:], y_win[t][:].indirect(kept_t[:]))
             nc.vector.tensor_tensor(prod[:, :V], y_win[t][:].indirect(drop1_t[:]), kk[:], ALU.mult)
             nc.vector.tensor_tensor(prod[:, V:], y_win[t][:].indirect(drop2_t[:]), kk[:], ALU.mult)
-            bounded = ring.tile([P, 2 * V], F32, name="bounded")
+            bounded = ring.tile([P, 2 * V], F32, name="bounded", tag="bounded")
             nc.scalar.activation(bounded[:], prod[:], ACT.Tanh)
             hw = keep.tile([P, 2 * V], F32, name=f"half_w{t}")
             nc.scalar.activation(hw[:], bounded[:], ACT.Exp, bias=-math.log(2.0))
             half_w.append(hw)
             for u in range(V // P):
-                dst = s_bank[t // 2][:, (t % 2) * V + u * P : (t % 2) * V + (u + 1) * P]
+                dst = s_bank[u][:, t * P : (t + 1) * P]
                 for d in range(2):
                     nc.tensor.matmul(dst, lhsT=hw[:, d * V + u * P : d * V + (u + 1) * P], rhs=ident[:], is_transpose=True,
                                      start=(d == 0), stop=(d == 1))
 
         def value_product(t):
-            grouped = keep.tile([P, PASSES * P * PACK], BF16, name=f"w2_bf{t}", align_bytes=64)
+            grouped = keep.tile([P, PASSES * P * PACK], BF16, name=f"w2_bf{t}", tag=f"w2_bf{(0, 1, 1, 0)[t]}", align_bytes=64)
             for o in range(PASSES):
                 cast(scopy if t < 2 else vcopy, w2_raw[o], t, grouped[:, o * P * PACK : (o + 1) * P * PACK])
             codes, scales = quantise(grouped[:], PASSES * P * PACK, f"w2_{t}")
             acc = mm.tile([P, S], F32, name="acc")
             for o in range(PASSES):
                 product(acc, o, codes[:, o * P : (o + 1) * P], scales[:, o * P : (o + 1) * P])
-            win = keep.tile([P, S], F32, name=f"yv_win{t}")
-            nc.scalar.activation(win[:], acc[:], ACT.Copy, scale=unit_t[t][:])
+            return acc
+
+        def value_window(t, acc):
+            win = ring.tile([P, S], F32, name=f"yv_win{t}", tag="bounded" if t < 2 else "late_values")
+            nc.scalar.activation(win[:], acc[:], ACT.Copy, scale=-0.5)
             yv_win.append(win)
 
         keys(0)
+        acc0 = value_product(0)
         keys(1)
-        value_product(0)
+        acc1 = value_product(1)
         keys(2)
-        value_product(1)
         keys(3)
-        value_product(2)
-        value_product(3)
-
-        log_s = keep.tile([P, PACK * V], F32, name="log_s")
+        value_window(0, acc0)
+        value_window(1, acc1)
+        acc2 = value_product(2)
+        acc3 = value_product(3)
+        log_s = keep.tile([P, 2, PACK * P], F32, name="log_s")
         for u in range(2):
-            nc.scalar.activation(log_s[:, u * 2 * V : (u + 1) * 2 * V], s_bank[u][:], ACT.Ln)
-        rho = []
-        for t in range(PACK):
-            tile = keep.tile([P, V], F32, name=f"rho{t}")
-            nc.scalar.activation(tile[:], log_s[:, t * V : (t + 1) * V], ACT.Tanh, scale=0.5)
-            rho.append(tile)
+            nc.scalar.activation(log_s[:, u, :], s_bank[u][:], ACT.Ln)
+        value_window(2, acc2)
+        value_window(3, acc3)
 
-        def values(t):
-            terms = ring.tile([P, 3 * V], F32, name="terms")
+        def values(t, n_banks):
+            terms = keep.tile([P, 3 * V], F32, name=f"terms{t}")
             nc.vector.tensor_copy(terms[:, :V], yv_win[t][:].indirect(kept_t[:]))
             nc.vector.tensor_tensor(terms[:, V : 2 * V], yv_win[t][:].indirect(drop1_t[:]), half_w[t][:, :V], ALU.mult)
             nc.vector.tensor_tensor(terms[:, 2 * V :], yv_win[t][:].indirect(drop2_t[:]), half_w[t][:, V:], ALU.mult)
-            n_bank = sums.tile([P, V], F32, name="n_bank")
-            for u in range(V // P):
-                for d in range(3):
-                    nc.tensor.matmul(n_bank[:, u * P : (u + 1) * P], lhsT=terms[:, d * V + u * P : d * V + (u + 1) * P], rhs=ident[:],
-                                     is_transpose=True, start=(d == 0), stop=(d == 2))
-            return n_bank
+            for d in range(3):
+                for u in range(V // P):
+                    nc.tensor.matmul(n_banks[u][:, (t % 2) * P : (t % 2 + 1) * P], lhsT=terms[:, d * V + u * P : d * V + (u + 1) * P],
+                                     rhs=ident[:], is_transpose=True, start=(d == 0), stop=(d == 2))
 
-        def merge(t, n_bank):
-            turned = ring.tile([P, V], F32, name="turned")
-            nc.vector.scalar_tensor_tensor(turned[:], rho[t][:], 1.0, n_bank[:], ALU.subtract, ALU.mult)
-            back = sums.tile([P, V], F32, name="back")
-            for u in range(V // P):
-                nc.tensor.transpose(back[:, u * P : (u + 1) * P], turned[:, u * P : (u + 1) * P], ident[:])
-            nc.scalar.activation(mv_win[t][:, :V], back[:], ACT.Copy, scale=-0.5)
+        n_low = [sums.tile([P, V], F32, name=f"n_low{u}") for u in range(2)]
+        values(0, n_low)
+        values(1, n_low)
+        n_high = [mm.tile([P, V], F32, name="acc") for u in range(2)]
+        values(2, n_high)
+        values(3, n_high)
 
-        for t in range(PACK):
-            merge(t, values(t))
+        rho = []
+        for pair in range(2):
+            tile = keep.tile([P, 2, V], F32, name=f"rho{pair}")
+            nc.scalar.activation(tile[:], log_s[:, :, pair * V : (pair + 1) * V], ACT.Tanh, scale=0.5)
+            rho.append(tile)
+
+        for pair, n_banks in enumerate((n_low, n_high)):
+            turned = []
+            for u in range(2):
+                tile = keep.tile([P, V], F32, name=f"turned{pair}{u}")
+                nc.vector.scalar_tensor_tensor(tile[:], rho[pair][:, u, :], 1.0, n_banks[u][:], ALU.subtract, ALU.mult)
+                turned.append(tile)
+            for e in range(2):
+                back = sums.tile([P, V], F32, name="s_bank", bufs=2)
+                for u in range(2):
+                    nc.tensor.transpose(back[:, u * P : (u + 1) * P], turned[u][:, e * P : (e + 1) * P], ident[:])
+                nc.scalar.activation(mv_win[2 * pair + e][:, :V], back[:], ACT.Copy, scale=unit_t[2 * pair + e][:])
 
         w3_bf = keep.tile([P, N * PACK], BF16, name="w3_bf", align_bytes=64)
         nc.scalar.copy(w3_bf[:].rearrange("p (c i j) -> p c j i", i=4, j=PACK), w3_raw[:].rearrange("p j (c i) -> p c j i", i=4))
@@ -216,7 +228,7 @@ def tile_picked_ywvmrg_read_p_kernel(tc, x_words, x_scales, w1, w2, pr, unit, w3
                 nc.vector.tensor_tensor(planes[:, t, :], mv_win[t][:].indirect(rd_t[:, r0 // 16 : (r0 + width) // 16]),
                                         pr_t[t][:, r0 : r0 + width], ALU.mult)
             hid_bf = keep.tile([P, width * PACK], BF16, name=f"hid_bf{c}", align_bytes=64)
-            nc.scalar.copy(hid_bf[:].rearrange("p (c i j) -> p c j i", i=4, j=PACK), planes[:].rearrange("p j (c i) -> p c j i", i=4))
+            (vcopy if c == len(CHUNKS) - 1 else scopy)(hid_bf[:].rearrange("p (c i j) -> p c j i", i=4, j=PACK), planes[:].rearrange("p j (c i) -> p c j i", i=4))
             codes, scales = quantise(hid_bf[:], width * PACK, f"hid{c}")
             acc = mm.tile([P, S], F32, name="acc")
             nc.tensor.matmul_mx(out=acc[:, :width], lhsT=w3_codes[:].bitcast(FP8X4), lhsT_scale=w3_scales[:],

@@ -54,21 +54,19 @@ def tile_picked_ywvmrg_read_p_kernel(tc, x_words, x_scales, w1, w2, pr, unit, w3
         for q in range(4):
             nc.sync.dma_start(scale_win[32 * q : 32 * q + 8, :].bitcast(I32), x_scales[:, 4 * q : 4 * q + 4, :].bitcast(I32))
         offs_t = load_list(offs, "offs_t")
+
+        def load_weight(w, o, name):
+            raw = keep.tile([P, PACK, H], F32, name=f"{name}_raw{o}")
+            nc.sync.dma_start(raw[:], w[512 * o : 512 * (o + 1), :].rearrange("(p j) c -> p j c", j=PACK))
+            return raw
+
+        w1_raw = [load_weight(w1, 0, "w1")]
         word_win.append(load_words(1))
-
-        def load_weight(w, name):
-            raws = []
-            for o in range(PASSES):
-                raw = keep.tile([P, PACK, H], F32, name=f"{name}_raw{o}")
-                nc.sync.dma_start(raw[:], w[512 * o : 512 * (o + 1), :].rearrange("(p j) c -> p j c", j=PACK))
-                raws.append(raw)
-            return raws
-
-        w1_raw = load_weight(w1, "w1")
         kept_t = load_list(kept, "kept_t")
         drop1_t = load_list(drop1, "drop1_t")
         drop2_t = load_list(drop2, "drop2_t")
-        w2_raw = load_weight(w2, "w2")
+        w1_raw.append(load_weight(w1, 1, "w1"))
+        w2_raw = [load_weight(w2, o, "w2") for o in range(PASSES)]
         pr_t = []
         for t in range(PACK):
             tile = keep.tile([P, U], F32, name=f"pr{t}")
@@ -112,75 +110,100 @@ def tile_picked_ywvmrg_read_p_kernel(tc, x_words, x_scales, w1, w2, pr, unit, w3
             nc.vector.quantize_mx(out=codes[:].bitcast(FP8X4), scales=scales[:], in_=src)
             return codes, scales
 
-        def product(acc, o, codes, scales):
-            nc.tensor.matmul_mx(out=acc[:], lhsT=codes.bitcast(FP8X4), lhsT_scale=scales, rhs=x_codes[o][:].bitcast(FP8X4),
-                                rhs_scale=x_bytes[4 * o : P, :], start=(o == 0), stop=(o == PASSES - 1))
+        def product(acc, o, codes, scales, cols=slice(0, S)):
+            nc.tensor.matmul_mx(out=acc[:], lhsT=codes.bitcast(FP8X4), lhsT_scale=scales, rhs=x_codes[o][:, cols].bitcast(FP8X4),
+                                rhs_scale=x_bytes[4 * o : P, cols], start=(o == 0), stop=(o == PASSES - 1))
 
         vcopy, scopy = nc.vector.tensor_copy, nc.scalar.copy
 
-        y_acc = [mm.tile([P, S], F32, name="acc") for t in range(PACK)]
+        halves = [slice(u * V, (u + 1) * V) for u in range(2)]
+        y_first = [sums.tile([P, V], F32, name=f"y_first{u}", tag=f"half_bank{u}") for u in range(2)]
+        y_acc = [None] + [mm.tile([P, S], F32, name="acc") for t in range(1, PACK)]
         for o, t in sorted(((o, t) for o in range(PASSES) for t in range(PACK)), key=lambda ot: (ot[1] + 2 * ot[0], -ot[0])):
-            grouped = keep.tile([P, P * PACK], BF16, name=f"w1_bf{o}{t}", align_bytes=64)
+            grouped = keep.tile([P, P * PACK], BF16, name=f"w1_bf{o}{t}", tag="stage0" if (o, t) == (1, 3) else f"w1_bf{o}{t}", align_bytes=64)
             cast(vcopy if t == 0 else scopy, w1_raw[o], t, grouped[:])
             codes, scales = quantise(grouped[:], P * PACK, f"w1_{o}{t}")
-            product(y_acc[t], o, codes[:], scales[:])
+            if t == 0:
+                for u in range(2):
+                    product(y_first[u], o, codes[:], scales[:], halves[u])
+            else:
+                product(y_acc[t], o, codes[:], scales[:])
         y_win = []
         for t in range(PACK):
             win = keep.tile([P, S], F32, name=f"y_win{t}")
-            (vcopy if t == 0 else scopy)(win[:], y_acc[t][:])
+            if t == 0:
+                for u in range(2):
+                    vcopy(win[:, halves[u]], y_first[u][:])
+            else:
+                scopy(win[:], y_acc[t][:])
             y_win.append(win)
 
         half_w = []
+        staged = []
+        prods = []
         yv_win = []
         s_bank = [sums.tile([P, 2 * V], F32, name="s_bank", bufs=2) for u in range(2)]
 
         def keys(t):
-            kk = keep.tile([P, V], F32, name=f"kk{t}")
-            prod = keep.tile([P, 2 * V], F32, name=f"prod{t}")
+            kk = keep.tile([P, V], F32, name=f"kk{t}", tag="stage1" if t == 0 else f"kk{t}", align_bytes=64)
+            if t < 3:
+                prods.append(keep.tile([P, 1 + t // 2, 2 * V], F32, name=f"prod{t}", tag="stage0" if t == 2 else f"prod{t}", align_bytes=64))
+            prod = prods[-1][:, max(t - 2, 0), :]
             nc.vector.tensor_copy(kk[:], y_win[t][:].indirect(kept_t[:]))
             nc.vector.tensor_tensor(prod[:, :V], y_win[t][:].indirect(drop1_t[:]), kk[:], ALU.mult)
             nc.vector.tensor_tensor(prod[:, V:], y_win[t][:].indirect(drop2_t[:]), kk[:], ALU.mult)
-            bounded = ring.tile([P, 2 * V], F32, name="bounded", tag="bounded")
-            nc.scalar.activation(bounded[:], prod[:], ACT.Tanh)
+            pieces = halves if t == PACK - 1 else [slice(0, 2 * V)]
+            bounded = []
+            for d, cols in enumerate(pieces):
+                tile = keep.tile([P, cols.stop - cols.start], F32, name=f"bounded{t}{d}", tag=f"bounded{t}{d}", align_bytes=64)
+                nc.scalar.activation(tile[:], prod[:, cols], ACT.Tanh)
+                bounded.append(tile)
             hw = keep.tile([P, 2 * V], F32, name=f"half_w{t}")
-            nc.scalar.activation(hw[:], bounded[:], ACT.Exp, bias=-math.log(2.0))
+            for tile, cols in zip(bounded, pieces):
+                nc.scalar.activation(hw[:, cols], tile[:], ACT.Exp, bias=-math.log(2.0))
             half_w.append(hw)
             for u in range(V // P):
-                dst = s_bank[u][:, t * P : (t + 1) * P]
+                dst = s_bank[t // 2][:, u * V + (t % 2) * P : u * V + (t % 2 + 1) * P]
                 for d in range(2):
                     nc.tensor.matmul(dst, lhsT=hw[:, d * V + u * P : d * V + (u + 1) * P], rhs=ident[:], is_transpose=True,
                                      start=(d == 0), stop=(d == 1))
 
-        def value_product(t):
-            grouped = keep.tile([P, PASSES * P * PACK], BF16, name=f"w2_bf{t}", tag=f"w2_bf{(0, 1, 1, 0)[t]}", align_bytes=64)
+        def value_codes(t):
+            if t < 3:
+                staged.append(keep.tile([P, 1 + t // 2, PASSES * P * PACK], BF16, name=f"w2_bf{t}", tag=f"stage{min(t, 1)}", align_bytes=64))
+            grouped = staged[-1][:, max(t - 2, 0), :]
             for o in range(PASSES):
-                cast(scopy if t < 2 else vcopy, w2_raw[o], t, grouped[:, o * P * PACK : (o + 1) * P * PACK])
-            codes, scales = quantise(grouped[:], PASSES * P * PACK, f"w2_{t}")
+                cast(scopy if (t, o) in ((0, 0), (1, 0), (1, 1)) else vcopy, w2_raw[o], t, grouped[:, o * P * PACK : (o + 1) * P * PACK])
+            return quantise(grouped, PASSES * P * PACK, f"w2_{t}")
+
+        def value_product(t, codes, scales):
             acc = mm.tile([P, S], F32, name="acc")
             for o in range(PASSES):
                 product(acc, o, codes[:, o * P : (o + 1) * P], scales[:, o * P : (o + 1) * P])
             return acc
 
         def value_window(t, acc):
-            win = ring.tile([P, S], F32, name=f"yv_win{t}", tag="bounded" if t < 2 else "late_values")
+            win = keep.tile([P, S], F32, name=f"yv_win{t}", tag="bounded30" if t == 1 else f"yv_win{t}", align_bytes=64)
             nc.scalar.activation(win[:], acc[:], ACT.Copy, scale=-0.5)
             yv_win.append(win)
 
         keys(0)
-        acc0 = value_product(0)
+        acc0 = value_product(0, *value_codes(0))
         keys(1)
-        acc1 = value_product(1)
+        staged1 = value_codes(1)
         keys(2)
-        keys(3)
         value_window(0, acc0)
+        acc1 = value_product(1, *staged1)
+        keys(3)
         value_window(1, acc1)
-        acc2 = value_product(2)
-        acc3 = value_product(3)
-        log_s = keep.tile([P, 2, PACK * P], F32, name="log_s")
-        for u in range(2):
-            nc.scalar.activation(log_s[:, u, :], s_bank[u][:], ACT.Ln)
-        value_window(2, acc2)
-        value_window(3, acc3)
+        acc2 = value_product(2, *value_codes(2))
+        acc3 = value_product(3, *value_codes(3))
+        log_s = []
+        for pair, acc in enumerate((acc2, acc3)):
+            tile = keep.tile([P, 2 * V], F32, name=f"log_s{pair}", tag=("bounded31", "log_s1")[pair], align_bytes=64)
+            nc.scalar.activation(tile[:], s_bank[pair][:], ACT.Ln)
+            log_s.append(tile)
+            value_window(2 + pair, acc)
 
         def values(t, n_banks):
             terms = keep.tile([P, 3 * V], F32, name=f"terms{t}")
@@ -192,7 +215,7 @@ def tile_picked_ywvmrg_read_p_kernel(tc, x_words, x_scales, w1, w2, pr, unit, w3
                     nc.tensor.matmul(n_banks[u][:, (t % 2) * P : (t % 2 + 1) * P], lhsT=terms[:, d * V + u * P : d * V + (u + 1) * P],
                                      rhs=ident[:], is_transpose=True, start=(d == 0), stop=(d == 2))
 
-        n_low = [sums.tile([P, V], F32, name=f"n_low{u}") for u in range(2)]
+        n_low = [sums.tile([P, V], F32, name=f"n_low{u}", tag=f"half_bank{u}") for u in range(2)]
         values(0, n_low)
         values(1, n_low)
         n_high = [mm.tile([P, V], F32, name="acc") for u in range(2)]
@@ -202,7 +225,7 @@ def tile_picked_ywvmrg_read_p_kernel(tc, x_words, x_scales, w1, w2, pr, unit, w3
         rho = []
         for pair in range(2):
             tile = keep.tile([P, 2, V], F32, name=f"rho{pair}")
-            nc.scalar.activation(tile[:], log_s[:, :, pair * V : (pair + 1) * V], ACT.Tanh, scale=0.5)
+            nc.scalar.activation(tile[:].rearrange("p u v -> p (u v)"), log_s[pair][:], ACT.Tanh, scale=0.5)
             rho.append(tile)
 
         for pair, n_banks in enumerate((n_low, n_high)):
@@ -217,7 +240,7 @@ def tile_picked_ywvmrg_read_p_kernel(tc, x_words, x_scales, w1, w2, pr, unit, w3
                     nc.tensor.transpose(back[:, u * P : (u + 1) * P], turned[u][:, e * P : (e + 1) * P], ident[:])
                 nc.scalar.activation(mv_win[2 * pair + e][:, :V], back[:], ACT.Copy, scale=unit_t[2 * pair + e][:])
 
-        w3_bf = keep.tile([P, N * PACK], BF16, name="w3_bf", align_bytes=64)
+        w3_bf = keep.tile([P, N * PACK], BF16, name="w3_bf", tag="log_s1", align_bytes=64)
         nc.scalar.copy(w3_bf[:].rearrange("p (c i j) -> p c j i", i=4, j=PACK), w3_raw[:].rearrange("p j (c i) -> p c j i", i=4))
         w3_codes, w3_scales = quantise(w3_bf[:], N * PACK, "w3")
 

@@ -207,13 +207,13 @@ def tile_picked_ywvmrg_read_p_kernel(tc, x_words, x_scales, w1, w2, pr, unit, w3
 
         def values(t, n_banks):
             terms = keep.tile([P, 3 * V], F32, name=f"terms{t}")
-            nc.vector.tensor_copy(terms[:, :V], yv_win[t][:].indirect(kept_t[:]))
-            nc.vector.tensor_tensor(terms[:, V : 2 * V], yv_win[t][:].indirect(drop1_t[:]), half_w[t][:, :V], ALU.mult)
-            nc.vector.tensor_tensor(terms[:, 2 * V :], yv_win[t][:].indirect(drop2_t[:]), half_w[t][:, V:], ALU.mult)
-            for d in range(3):
+            nc.vector.tensor_tensor(terms[:, :V], yv_win[t][:].indirect(drop1_t[:]), half_w[t][:, :V], ALU.mult)
+            nc.vector.tensor_tensor(terms[:, V : 2 * V], yv_win[t][:].indirect(drop2_t[:]), half_w[t][:, V:], ALU.mult)
+            nc.vector.tensor_tensor(terms[:, 2 * V :], yv_win[t][:].indirect(kept_t[:]), terms[:, :V], ALU.add)
+            for d in (1, 2):
                 for u in range(V // P):
                     nc.tensor.matmul(n_banks[u][:, (t % 2) * P : (t % 2 + 1) * P], lhsT=terms[:, d * V + u * P : d * V + (u + 1) * P],
-                                     rhs=ident[:], is_transpose=True, start=(d == 0), stop=(d == 2))
+                                     rhs=ident[:], is_transpose=True, start=(d == 1), stop=(d == 2))
 
         n_low = [sums.tile([P, V], F32, name=f"n_low{u}", tag=f"half_bank{u}") for u in range(2)]
         values(0, n_low)

@@ -139,13 +139,12 @@ def tile_picked_ywvmrg_read_p_kernel(tc, x_words, x_scales, w1, w2, pr, unit, w3
             y_win.append(win)
 
         half_w = []
-        staged = []
         prods = []
         yv_win = []
         s_bank = [sums.tile([P, 2 * V], F32, name="s_bank", bufs=2) for u in range(2)]
 
         def keys(t):
-            kk = keep.tile([P, V], F32, name=f"kk{t}", tag="stage1" if t == 0 else f"kk{t}", align_bytes=64)
+            kk = keep.tile([P, V], F32, name=f"kk{t}", tag=f"stage{t + 1}" if t < 2 else f"kk{t}", align_bytes=64)
             if t < 3:
                 prods.append(keep.tile([P, 1 + t // 2, 2 * V], F32, name=f"prod{t}", tag="stage0" if t == 2 else f"prod{t}", align_bytes=64))
             prod = prods[-1][:, max(t - 2, 0), :]
@@ -169,12 +168,10 @@ def tile_picked_ywvmrg_read_p_kernel(tc, x_words, x_scales, w1, w2, pr, unit, w3
                                      start=(d == 0), stop=(d == 1))
 
         def value_codes(t):
-            if t < 3:
-                staged.append(keep.tile([P, 1 + t // 2, PASSES * P * PACK], BF16, name=f"w2_bf{t}", tag=f"stage{min(t, 1)}", align_bytes=64))
-            grouped = staged[-1][:, max(t - 2, 0), :]
+            grouped = keep.tile([P, PASSES * P * PACK], BF16, name=f"w2_bf{t}", tag=f"stage{(0, 1, 2, 1)[t]}", align_bytes=64)
             for o in range(PASSES):
-                cast(scopy if (t, o) in ((0, 0), (1, 0), (1, 1)) else vcopy, w2_raw[o], t, grouped[:, o * P * PACK : (o + 1) * P * PACK])
-            return quantise(grouped, PASSES * P * PACK, f"w2_{t}")
+                cast(scopy if (t, o) in ((0, 0), (1, 0), (1, 1), (2, 0), (2, 1)) else vcopy, w2_raw[o], t, grouped[:, o * P * PACK : (o + 1) * P * PACK])
+            return quantise(grouped[:], PASSES * P * PACK, f"w2_{t}")
 
         def value_product(t, codes, scales):
             acc = mm.tile([P, S], F32, name="acc")
@@ -191,12 +188,13 @@ def tile_picked_ywvmrg_read_p_kernel(tc, x_words, x_scales, w1, w2, pr, unit, w3
         acc0 = value_product(0, *value_codes(0))
         keys(1)
         staged1 = value_codes(1)
+        staged2 = value_codes(2)
         keys(2)
         value_window(0, acc0)
         acc1 = value_product(1, *staged1)
         keys(3)
         value_window(1, acc1)
-        acc2 = value_product(2, *value_codes(2))
+        acc2 = value_product(2, *staged2)
         acc3 = value_product(3, *value_codes(3))
         log_s = []
         for pair, acc in enumerate((acc2, acc3)):

from contextlib import ExitStack

import math

import concourse.mybir as mybir
from concourse.masks import make_identity

K, T, S, N, H, V, U = 1024, 2048, 512, 128, 512, 256, 1024
FLOPS = 2 * (2 * K * H * S + H * N * U)

F32 = mybir.dt.float32
BF16 = mybir.dt.bfloat16
I32 = mybir.dt.int32
U32 = mybir.dt.uint32
U16 = mybir.dt.uint16
U8 = mybir.dt.uint8
FP8X4 = mybir.dt.float8_e4m3fn_x4
ACT = mybir.ActivationFunctionType
ALU = mybir.AluOpType

P = 128
PACK = 4
PASSES = K // (P * PACK)
CHUNKS = (256, 256, 256, 128, 128)
WINDOW = max(CHUNKS) + 16


def tile_picked_ywvmrg_read_p_kernel(tc, x_words, x_scales, w1, w2, pr, unit, w3, offs, kept, drop1, drop2, rd, out):
    nc = tc.nc
    with ExitStack() as ctx:
        lists = ctx.enter_context(tc.tile_pool(name="lists", bufs=1))
        keep = ctx.enter_context(tc.tile_pool(name="keep", bufs=1))
        ring = ctx.enter_context(tc.tile_pool(name="ring", bufs=2))
        mm = ctx.enter_context(tc.psum_pool(name="mm", bufs=4))
        sums = ctx.enter_context(tc.psum_pool(name="sums", bufs=1))

        def load_list(src, name):
            tile = lists.tile(list(src.shape), U16, name=name)
            nc.sync.dma_start(tile[:], src)
            return tile

        def by_slot(src):
            return src.rearrange("(b t i) n -> t b i n", t=PACK, i=8)

        scale_win = keep.tile([P, T], U8, name="scale_win", align_bytes=64)
        nc.vector.memset(scale_win[:].bitcast(I32), 0)

        def load_words(o):
            win = keep.tile([P, T], I32, name=f"word_win{o}", align_bytes=64)
            nc.sync.dma_start(win[:], x_words[o].rearrange("p c r -> p (c r)").bitcast(I32))
            return win

        word_win = [load_words(0)]
        for q in range(4):
            nc.sync.dma_start(scale_win[32 * q : 32 * q + 8, :].bitcast(I32), x_scales[:, 4 * q : 4 * q + 4, :].bitcast(I32))
        offs_t = load_list(offs, "offs_t")

        def load_weight(w, o, name):
            raw = keep.tile([P, PACK, H], F32, name=f"{name}_raw{o}")
            nc.sync.dma_start(raw[:], w[512 * o : 512 * (o + 1), :].rearrange("(p j) c -> p j c", j=PACK))
            return raw

        w1_raw = [load_weight(w1, 0, "w1")]
        word_win.append(load_words(1))
        kept_t = load_list(kept, "kept_t")
        drop1_t = load_list(drop1, "drop1_t")
        drop2_t = load_list(drop2, "drop2_t")
        w1_raw.append(load_weight(w1, 1, "w1"))
        w2_raw = [load_weight(w2, o, "w2") for o in range(PASSES)]
        pr_t = []
        for t in range(PACK):
            tile = keep.tile([P, U], F32, name=f"pr{t}")
            nc.sync.dma_start(tile[:], by_slot(pr)[t])
            pr_t.append(tile)
        rd_t = load_list(rd, "rd_t")
        unit_t = []
        with nc.allow_non_contiguous_dma(reason="one value a partition"):
            for t in range(PACK):
                tile = keep.tile([P, 1], F32, name=f"unit{t}")
                nc.sync.dma_start(tile[:], by_slot(unit)[t])
                unit_t.append(tile)
        w3_raw = keep.tile([P, PACK, N], F32, name="w3_raw")
        for t in range(PACK):
            nc.sync.dma_start(w3_raw[:, t, :], by_slot(w3)[t])

        ident = keep.tile([P, P], F32, name="ident")
        make_identity(nc, ident[:])
        mv_win = []
        for t in range(PACK):
            win = keep.tile([P, WINDOW], F32, name=f"mv_win{t}")
            nc.gpsimd.memset(win[:, V:], 0.0)
            mv_win.append(win)

        x_codes = []
        for o in range(PASSES):
            codes = keep.tile([P, S], U32, name=f"x_codes{o}", align_bytes=64)
            nc.vector.tensor_copy(codes[:], word_win[o][:].bitcast(U32).indirect(offs_t[:]))
            x_codes.append(codes)
            if o == 0:
                x_bytes = keep.tile([P, S], U8, name="x_bytes", align_bytes=64)
                nc.vector.tensor_copy(x_bytes[:], scale_win[:].indirect(offs_t[:]))

        def cast(engine_copy, raw, t, dst):
            src = raw[:].rearrange("p j (b t h i) -> p t b h j i", t=PACK, h=2, i=4)[:, t]
            engine_copy(dst.rearrange("p (b h i j) -> p b h j i", h=2, i=4, j=PACK), src)

        def quantise(src, width, name):
            codes = keep.tile([P, width // PACK], U32, name=name + "_codes", align_bytes=64)
            scales = keep.tile([P, width // PACK], U8, name=name + "_scales", align_bytes=64)
            nc.vector.quantize_mx(out=codes[:].bitcast(FP8X4), scales=scales[:], in_=src)
            return codes, scales

        def product(acc, o, codes, scales, cols=slice(0, S)):
            nc.tensor.matmul_mx(out=acc[:], lhsT=codes.bitcast(FP8X4), lhsT_scale=scales, rhs=x_codes[o][:, cols].bitcast(FP8X4),
                                rhs_scale=x_bytes[4 * o : P, cols], start=(o == 0), stop=(o == PASSES - 1))

        vcopy, scopy = nc.vector.tensor_copy, nc.scalar.copy

        halves = [slice(u * V, (u + 1) * V) for u in range(2)]
        y_first = [sums.tile([P, V], F32, name=f"y_first{u}", tag=f"half_bank{u}") for u in range(2)]
        y_acc = [None] + [mm.tile([P, S], F32, name="acc") for t in range(1, PACK)]
        for o, t in sorted(((o, t) for o in range(PASSES) for t in range(PACK)), key=lambda ot: (ot[1] + 2 * ot[0], -ot[0])):
            grouped = keep.tile([P, P * PACK], BF16, name=f"w1_bf{o}{t}", tag="stage0" if (o, t) == (1, 3) else f"w1_bf{o}{t}", align_bytes=64)
            cast(vcopy if t == 0 else scopy, w1_raw[o], t, grouped[:])
            codes, scales = quantise(grouped[:], P * PACK, f"w1_{o}{t}")
            if t == 0:
                for u in range(2):
                    product(y_first[u], o, codes[:], scales[:], halves[u])
            else:
                product(y_acc[t], o, codes[:], scales[:])
        y_win = []
        for t in range(PACK):
            win = keep.tile([P, S], F32, name=f"y_win{t}")
            if t == 0:
                for u in range(2):
                    vcopy(win[:, halves[u]], y_first[u][:])
            else:
                scopy(win[:], y_acc[t][:])
            y_win.append(win)

        half_w = []
        prods = []
        yv_win = []
        s_bank = [sums.tile([P, 2 * V], F32, name="s_bank", bufs=2) for u in range(2)]

        def keys(t):
            kk = keep.tile([P, V], F32, name=f"kk{t}", tag=f"stage{t + 1}" if t < 2 else f"kk{t}", align_bytes=64)
            if t < 3:
                prods.append(keep.tile([P, 1 + t // 2, 2 * V], F32, name=f"prod{t}", tag="stage0" if t == 2 else f"prod{t}", align_bytes=64))
            prod = prods[-1][:, max(t - 2, 0), :]
            nc.vector.tensor_copy(kk[:], y_win[t][:].indirect(kept_t[:]))
            nc.vector.tensor_tensor(prod[:, :V], y_win[t][:].indirect(drop1_t[:]), kk[:], ALU.mult)
            nc.vector.tensor_tensor(prod[:, V:], y_win[t][:].indirect(drop2_t[:]), kk[:], ALU.mult)
            pieces = halves if t == PACK - 1 else [slice(0, 2 * V)]
            bounded = []
            for d, cols in enumerate(pieces):
                tile = keep.tile([P, cols.stop - cols.start], F32, name=f"bounded{t}{d}", tag=f"bounded{t}{d}", align_bytes=64)
                nc.scalar.activation(tile[:], prod[:, cols], ACT.Tanh)
                bounded.append(tile)
            hw = keep.tile([P, 2 * V], F32, name=f"half_w{t}")
            for tile, cols in zip(bounded, pieces):
                nc.scalar.activation(hw[:, cols], tile[:], ACT.Exp, bias=-math.log(2.0))
            half_w.append(hw)
            for u in range(V // P):
                dst = s_bank[t // 2][:, u * V + (t % 2) * P : u * V + (t % 2 + 1) * P]
                for d in range(2):
                    nc.tensor.matmul(dst, lhsT=hw[:, d * V + u * P : d * V + (u + 1) * P], rhs=ident[:], is_transpose=True,
                                     start=(d == 0), stop=(d == 1))

        def value_codes(t):
            grouped = keep.tile([P, PASSES * P * PACK], BF16, name=f"w2_bf{t}", tag=f"stage{(0, 1, 2, 1)[t]}", align_bytes=64)
            for o in range(PASSES):
                cast(scopy if (t, o) in ((0, 0), (1, 0), (1, 1), (2, 0), (2, 1)) else vcopy, w2_raw[o], t, grouped[:, o * P * PACK : (o + 1) * P * PACK])
            return quantise(grouped[:], PASSES * P * PACK, f"w2_{t}")

        def value_product(t, codes, scales):
            acc = mm.tile([P, S], F32, name="acc")
            for o in range(PASSES):
                product(acc, o, codes[:, o * P : (o + 1) * P], scales[:, o * P : (o + 1) * P])
            return acc

        def value_window(t, acc):
            win = keep.tile([P, S], F32, name=f"yv_win{t}", tag="bounded30" if t == 1 else f"yv_win{t}", align_bytes=64)
            nc.scalar.activation(win[:], acc[:], ACT.Copy, scale=-0.5)
            yv_win.append(win)

        keys(0)
        acc0 = value_product(0, *value_codes(0))
        keys(1)
        staged1 = value_codes(1)
        staged2 = value_codes(2)
        keys(2)
        value_window(0, acc0)
        acc1 = value_product(1, *staged1)
        keys(3)
        value_window(1, acc1)
        acc2 = value_product(2, *staged2)
        acc3 = value_product(3, *value_codes(3))
        log_s = []
        for pair, acc in enumerate((acc2, acc3)):
            tile = keep.tile([P, 2 * V], F32, name=f"log_s{pair}", tag=("bounded31", "log_s1")[pair], align_bytes=64)
            nc.scalar.activation(tile[:], s_bank[pair][:], ACT.Ln)
            log_s.append(tile)
            value_window(2 + pair, acc)

        def values(t, n_banks):
            terms = keep.tile([P, 3 * V], F32, name=f"terms{t}")
            nc.vector.tensor_tensor(terms[:, :V], yv_win[t][:].indirect(drop1_t[:]), half_w[t][:, :V], ALU.mult)
            nc.vector.tensor_tensor(terms[:, V : 2 * V], yv_win[t][:].indirect(drop2_t[:]), half_w[t][:, V:], ALU.mult)
            nc.vector.tensor_tensor(terms[:, 2 * V :], yv_win[t][:].indirect(kept_t[:]), terms[:, :V], ALU.add)
            for d in (1, 2):
                for u in range(V // P):
                    nc.tensor.matmul(n_banks[u][:, (t % 2) * P : (t % 2 + 1) * P], lhsT=terms[:, d * V + u * P : d * V + (u + 1) * P],
                                     rhs=ident[:], is_transpose=True, start=(d == 1), stop=(d == 2))

        n_low = [sums.tile([P, V], F32, name=f"n_low{u}", tag=f"half_bank{u}") for u in range(2)]
        values(0, n_low)
        values(1, n_low)
        n_high = [mm.tile([P, V], F32, name="acc") for u in range(2)]
        values(2, n_high)
        values(3, n_high)

        rho = []
        for pair in range(2):
            tile = keep.tile([P, 2, V], F32, name=f"rho{pair}")
            nc.scalar.activation(tile[:].rearrange("p u v -> p (u v)"), log_s[pair][:], ACT.Tanh, scale=0.5)
            rho.append(tile)

        for pair, n_banks in enumerate((n_low, n_high)):
            turned = []
            for u in range(2):
                tile = keep.tile([P, V], F32, name=f"turned{pair}{u}")
                nc.vector.scalar_tensor_tensor(tile[:], rho[pair][:, u, :], 1.0, n_banks[u][:], ALU.subtract, ALU.mult)
                turned.append(tile)
            for e in range(2):
                back = sums.tile([P, V], F32, name="s_bank", bufs=2)
                for u in range(2):
                    nc.tensor.transpose(back[:, u * P : (u + 1) * P], turned[u][:, e * P : (e + 1) * P], ident[:])
                nc.scalar.activation(mv_win[2 * pair + e][:, :V], back[:], ACT.Copy, scale=unit_t[2 * pair + e][:])

        w3_bf = keep.tile([P, N * PACK], BF16, name="w3_bf", tag="log_s1", align_bytes=64)
        nc.scalar.copy(w3_bf[:].rearrange("p (c i j) -> p c j i", i=4, j=PACK), w3_raw[:].rearrange("p j (c i) -> p c j i", i=4))
        w3_codes, w3_scales = quantise(w3_bf[:], N * PACK, "w3")

        r0 = 0
        for c, width in enumerate(CHUNKS):
            planes = keep.tile([P, PACK, width], F32, name=f"planes{c}")
            for t in range(PACK):
                nc.vector.tensor_tensor(planes[:, t, :], mv_win[t][:].indirect(rd_t[:, r0 // 16 : (r0 + width) // 16]),
                                        pr_t[t][:, r0 : r0 + width], ALU.mult)
            hid_bf = keep.tile([P, width * PACK], BF16, name=f"hid_bf{c}", align_bytes=64)
            (vcopy if c == len(CHUNKS) - 1 else scopy)(hid_bf[:].rearrange("p (c i j) -> p c j i", i=4, j=PACK), planes[:].rearrange("p j (c i) -> p c j i", i=4))
            codes, scales = quantise(hid_bf[:], width * PACK, f"hid{c}")
            acc = mm.tile([P, S], F32, name="acc")
            nc.tensor.matmul_mx(out=acc[:, :width], lhsT=w3_codes[:].bitcast(FP8X4), lhsT_scale=w3_scales[:],
                                rhs=codes[:].bitcast(FP8X4), rhs_scale=scales[:], start=True, stop=True)
            result = keep.tile([P, width], F32, name=f"result{c}")
            nc.scalar.copy(result[:], acc[:, :width])
            nc.sync.dma_start(out[:, r0 : r0 + width], result[:])
            r0 += width
